import numpy as np
import ml_dtypes

BF16 = ml_dtypes.bfloat16


def bf(x):
    return np.asarray(x, np.float32).astype(BF16)


def f32(x):
    return np.asarray(x, np.float32)


def f64(x):
    return np.asarray(x).astype(np.float64)


def striped(idx):
    return np.tile(idx.reshape(-1, 16).T, (8, 1))


S, K, M, N, D, V = 512, 128, 128, 512, 2, 256


def setup_inputs():
    return {"table": bf(np.random.standard_normal((S, K))), "w": bf(np.random.standard_normal((K, M)) / np.sqrt(D * K)), "b": f32(0.5 * np.random.standard_normal((M, 1))), "offs": striped(np.random.permutation(np.tile(np.arange(S), 2))[:N])}


def reference(table, w, b, offs):
    idx = offs[:16].T.reshape(-1)
    x = f64(table)[idx].T
    y = f64(w).T @ sum(x[:, t * V : (t + 1) * V] for t in range(D))
    return y + f64(b)

@@ -1,0 +1,46 @@
+import concourse.mybir as mybir
+from concourse.masks import make_identity
+
+BF16, F32, U16 = mybir.dt.bfloat16, mybir.dt.float32, mybir.dt.uint16
+P = 128
+NODES = 512
+OUT_NODES = 256
+NEIGHBOURS = 2
+BLOCKS = NODES // P
+PER_COLUMN = 16
+
+FLOPS = 2 * NEIGHBOURS * OUT_NODES * P * P
+
+
+def tile_gather_matmul_kernel(tc, table, w, b, offs, out):
+    nc = tc.nc
+    piece_columns = OUT_NODES // PER_COLUMN
+    with (
+        tc.tile_pool(name="held", bufs=1) as held,
+        tc.psum_pool(name="psum", bufs=1) as psum,
+    ):
+        rows = held.tile([P, BLOCKS, P], BF16, name="rows")
+        nc.sync.dma_start(rows[:], table.rearrange("(a p) k -> p a k", p=P))
+        offsets = held.tile([P, NEIGHBOURS * piece_columns], U16, name="offsets")
+        nc.sync.dma_start(offsets[:], offs)
+        weights = held.tile([P, P], BF16, name="weights")
+        nc.scalar.dma_start(weights[:], w)
+        bias = held.tile([P, 1], F32, name="bias")
+        nc.scalar.dma_start(bias[:], b)
+        identity = held.tile([P, P], BF16, name="identity")
+        make_identity(nc, identity[:])
+
+        flipped = psum.tile([P, NODES], BF16, name="flipped")
+        for a in range(BLOCKS):
+            nc.tensor.transpose(flipped[:, a * P : (a + 1) * P], rows[:, a, :], identity[:])
+        features = held.tile([P, NODES], BF16, name="features")
+        nc.vector.tensor_copy(features[:], flipped[:])
+
+        summed = psum.tile([P, OUT_NODES], F32, name="summed")
+        for t in range(NEIGHBOURS):
+            picked = features[:].indirect(offsets[:, t * piece_columns : (t + 1) * piece_columns])
+            nc.tensor.matmul(summed[:], weights[:], picked, start=(t == 0), stop=(t == NEIGHBOURS - 1))
+
+        result = held.tile([P, OUT_NODES], F32, name="result")
+        nc.vector.tensor_scalar_add(result[:], summed[:], bias[:])
+        nc.sync.dma_start(out, result[:])

@@ -15,6 +15,8 @@ FLOPS = 2 * NEIGHBOURS * OUT_NODES * P * P
 def tile_gather_matmul_kernel(tc, table, w, b, offs, out):
     nc = tc.nc
     piece_columns = OUT_NODES // PER_COLUMN
+    half_nodes = OUT_NODES // 2
+    half_columns = half_nodes // PER_COLUMN
     with (
         tc.tile_pool(name="held", bufs=1) as held,
         tc.psum_pool(name="psum", bufs=1) as psum,
@@ -36,11 +38,12 @@ def tile_gather_matmul_kernel(tc, table, w, b, offs, out):
         features = held.tile([P, NODES], BF16, name="features")
         nc.vector.tensor_copy(features[:], flipped[:])
 
-        summed = psum.tile([P, OUT_NODES], F32, name="summed")
-        for t in range(NEIGHBOURS):
-            picked = features[:].indirect(offsets[:, t * piece_columns : (t + 1) * piece_columns])
-            nc.tensor.matmul(summed[:], weights[:], picked, start=(t == 0), stop=(t == NEIGHBOURS - 1))
-
-        result = held.tile([P, OUT_NODES], F32, name="result")
-        nc.vector.tensor_scalar_add(result[:], summed[:], bias[:])
-        nc.sync.dma_start(out, result[:])
+        for h in range(2):
+            summed = psum.tile([P, half_nodes], F32, name=f"summed{h}")
+            for t in range(NEIGHBOURS):
+                first = t * piece_columns + h * half_columns
+                picked = features[:].indirect(offsets[:, first : first + half_columns])
+                nc.tensor.matmul(summed[:], weights[:], picked, start=(t == 0), stop=(t == NEIGHBOURS - 1))
+            result = held.tile([P, half_nodes], F32, name=f"result{h}")
+            nc.vector.tensor_scalar_add(result[:], summed[:], bias[:])
+            nc.sync.dma_start(out[:, h * half_nodes : (h + 1) * half_nodes], result[:])

@@ -21,28 +21,30 @@ def tile_gather_matmul_kernel(tc, table, w, b, offs, out):
         tc.tile_pool(name="held", bufs=1) as held,
         tc.psum_pool(name="psum", bufs=1) as psum,
     ):
-        rows = held.tile([P, BLOCKS, P], BF16, name="rows")
-        nc.sync.dma_start(rows[:], table.rearrange("(a p) k -> p a k", p=P))
+        rows = held.tile([P, 2, 2, P], BF16, name="rows")
+        nc.sync.dma_start(rows[:], table.rearrange("(h p a) k -> p h a k", p=P, a=2))
         offsets = held.tile([P, NEIGHBOURS * piece_columns], U16, name="offsets")
         nc.sync.dma_start(offsets[:], offs)
         weights = held.tile([P, P], BF16, name="weights")
-        nc.scalar.dma_start(weights[:], w)
+        nc.sync.dma_start(weights[:], w)
         bias = held.tile([P, 1], F32, name="bias")
-        nc.scalar.dma_start(bias[:], b)
+        nc.sync.dma_start(bias[:], b)
         identity = held.tile([P, P], BF16, name="identity")
         make_identity(nc, identity[:])
 
-        flipped = psum.tile([P, NODES], BF16, name="flipped")
-        for a in range(BLOCKS):
-            nc.tensor.transpose(flipped[:, a * P : (a + 1) * P], rows[:, a, :], identity[:])
-        features = held.tile([P, NODES], BF16, name="features")
-        nc.vector.tensor_copy(features[:], flipped[:])
+        features = held.tile([P, 2, P, 2], BF16, name="features")
+        for h in range(2):
+            flipped = psum.tile([P, 2, P], BF16, name=f"flipped{h}")
+            for a in range(2):
+                nc.tensor.transpose(flipped[:, a, :], rows[:, h, a, :], identity[:])
+            nc.vector.tensor_copy(features[:, h, :, :], flipped[:].rearrange("k a p -> k p a"))
+        nodes = features[:].rearrange("k h p a -> k (h p a)")
 
         for h in range(2):
             summed = psum.tile([P, half_nodes], F32, name=f"summed{h}")
             for t in range(NEIGHBOURS):
                 first = t * piece_columns + h * half_columns
-                picked = features[:].indirect(offsets[:, first : first + half_columns])
+                picked = nodes.indirect(offsets[:, first : first + half_columns])
                 nc.tensor.matmul(summed[:], weights[:], picked, start=(t == 0), stop=(t == NEIGHBOURS - 1))
             result = held.tile([P, half_nodes], F32, name=f"result{h}")
             nc.vector.tensor_scalar_add(result[:], summed[:], bias[:])

import concourse.mybir as mybir
from concourse.masks import make_identity

BF16, F32, U16 = mybir.dt.bfloat16, mybir.dt.float32, mybir.dt.uint16
P = 128
NODES = 512
OUT_NODES = 256
NEIGHBOURS = 2
BLOCKS = NODES // P
PER_COLUMN = 16

FLOPS = 2 * NEIGHBOURS * OUT_NODES * P * P


def tile_gather_matmul_kernel(tc, table, w, b, offs, out):
    nc = tc.nc
    piece_columns = OUT_NODES // PER_COLUMN
    half_nodes = OUT_NODES // 2
    half_columns = half_nodes // PER_COLUMN
    with (
        tc.tile_pool(name="held", bufs=1) as held,
        tc.psum_pool(name="psum", bufs=1) as psum,
    ):
        rows = held.tile([P, 2, 2, P], BF16, name="rows")
        nc.sync.dma_start(rows[:], table.rearrange("(h p a) k -> p h a k", p=P, a=2))
        offsets = held.tile([P, NEIGHBOURS * piece_columns], U16, name="offsets")
        nc.sync.dma_start(offsets[:], offs)
        weights = held.tile([P, P], BF16, name="weights")
        nc.sync.dma_start(weights[:], w)
        bias = held.tile([P, 1], F32, name="bias")
        nc.sync.dma_start(bias[:], b)
        identity = held.tile([P, P], BF16, name="identity")
        make_identity(nc, identity[:])

        features = held.tile([P, 2, P, 2], BF16, name="features")
        for h in range(2):
            flipped = psum.tile([P, 2, P], BF16, name=f"flipped{h}")
            for a in range(2):
                nc.tensor.transpose(flipped[:, a, :], rows[:, h, a, :], identity[:])
            nc.vector.tensor_copy(features[:, h, :, :], flipped[:].rearrange("k a p -> k p a"))
        nodes = features[:].rearrange("k h p a -> k (h p a)")

        for h in range(2):
            summed = psum.tile([P, half_nodes], F32, name=f"summed{h}")
            for t in range(NEIGHBOURS):
                first = t * piece_columns + h * half_columns
                picked = nodes.indirect(offsets[:, first : first + half_columns])
                nc.tensor.matmul(summed[:], weights[:], picked, start=(t == 0), stop=(t == NEIGHBOURS - 1))
            result = held.tile([P, half_nodes], F32, name=f"result{h}")
            nc.vector.tensor_scalar_add(result[:], summed[:], bias[:])
            nc.sync.dma_start(out[:, h * half_nodes : (h + 1) * half_nodes], result[:])
